import numpy as np
import ml_dtypes


def mxq(x, axis, fmt="e4m3"):
    dtype, down = {"e4m3": (ml_dtypes.float8_e4m3fn, 7), "e5m2": (ml_dtypes.float8_e5m2, 14)}[fmt]
    v = np.moveaxis(np.asarray(x, np.float32).astype(ml_dtypes.bfloat16).astype(np.float64), axis, -1)
    blocks = v.reshape(v.shape[:-1] + (-1, 32))
    amax = np.abs(blocks).max(-1, keepdims=True)
    byte = np.maximum(np.where(amax > 0, np.frexp(amax)[1] - 1 + 127, 0) - down, 1)
    scale = np.exp2(byte - 127.0)
    codes = (blocks / scale).astype(np.float32).astype(dtype).astype(np.float64)
    return np.moveaxis((codes * scale).reshape(v.shape), -1, axis)


WIDE = False


def mx_kscale(k):
    if not WIDE:
        return np.ones(k)
    levels = np.array([10, -10, 5, -5, 0])
    if k % 512:
        return np.exp2(np.random.permutation(np.resize(levels, k // 32))).repeat(32)
    a = np.empty((k // 512, 16))
    for p in range(k // 512):
        a[p, :8] = np.random.permutation(np.resize(levels, 8))
        for g in range(8):
            far = levels[np.abs(levels - a[p, g]) >= 10]
            a[p, g + 8] = far[np.random.randint(len(far))]
    return np.exp2(a.ravel()).repeat(32)


def f64(x):
    return np.asarray(x).astype(np.float64)


def striped8(idx):
    return np.asarray(idx).reshape(8, -1, 16).transpose(0, 2, 1).reshape(128, -1).astype(np.uint16)


def unstriped8(offs):
    return offs.reshape(8, 16, -1).transpose(0, 2, 1).reshape(8, -1).astype(np.int64)


def pick8(x, idx, run):
    r = np.arange(len(x))
    return x[r[:, None], idx[r % (8 * run) // run]]


E2M1 = np.array([0.0, 0.5, 1.0, 1.5, 2.0, 3.0, 4.0, 6.0, -0.0, -0.5, -1.0, -1.5, -2.0, -3.0, -4.0, -6.0])


def pack_weight(w, fmt):
    k, n = w.shape
    w = f64(np.asarray(w, np.float32).astype(ml_dtypes.bfloat16)).reshape(k // 32, 32, n)
    amax = np.abs(w).max(1)
    if fmt == "e4m3":
        byte = np.frexp(amax)[1] - 1 + 127 - 7
    else:
        mant, ex = np.frexp(amax / 6.0)
        byte = np.where(mant > 0.5, ex, ex - 1) + 127
    byte = np.clip(np.where(amax > 0, byte, 1), 1, 254)
    scaled = (w * np.exp2(127.0 - byte)[:, None, :]).reshape(k, n).astype(np.float32)
    by_word = np.ascontiguousarray(scaled.reshape(k // 512, 128, 4, n).transpose(0, 1, 3, 2))
    if fmt == "e4m3":
        words = by_word.astype(ml_dtypes.float8_e4m3fn).view(np.uint8)
    else:
        c = by_word.astype(ml_dtypes.float4_e2m1fn).view(np.uint8) & 0xF
        words = (c[..., 0::2] | (c[..., 1::2] << 4)).reshape(k // 512, 128, 2 * n)
    return np.ascontiguousarray(words), np.ascontiguousarray(byte.astype(np.uint8).reshape(k // 512, 16, n))


def unpack_weight(words, scales, fmt):
    g, _, n = scales.shape
    words = np.ascontiguousarray(words).reshape(g, 128, n, -1)
    if fmt == "e4m3":
        vals = words.view(ml_dtypes.float8_e4m3fn).astype(np.float64)
    else:
        nib = np.empty((g, 128, n, 4), np.uint8)
        nib[..., 0::2] = words & 0xF
        nib[..., 1::2] = words >> 4
        vals = E2M1[nib]
    vals = vals * np.repeat(np.exp2(scales.astype(np.float64) - 127.0), 8, axis=1)[..., None]
    return vals.transpose(0, 1, 3, 2).reshape(g * 512, n)


D, K, T, U, I, Q = 512, 512, 1024, 1024, 512, 128


def setup_inputs():
    n = np.random.standard_normal
    idx = np.stack([np.random.permutation(T)[:I] for _ in range(8)])
    idx2 = np.stack([np.random.permutation(U)[:I] for _ in range(8)])
    idx3 = np.stack([np.random.permutation(U)[:I] for _ in range(8)])
    idx4 = np.stack([np.random.permutation(T)[:I] for _ in range(8)])
    idx5 = np.stack([np.random.permutation(U)[:I] for _ in range(8)])
    idx6 = np.stack([np.random.permutation(T)[:I] for _ in range(8)])
    fd = mx_kscale(D)
    fk = mx_kscale(K)
    wqp = pack_weight(n((D, K)) * 1.0 / np.sqrt(D) * fd[:, None] * fk, "e4m3")
    keysp = pack_weight(n((K, T)) * 1.0 / np.sqrt(K) / fk[:, None], "e2m1")
    notesp = pack_weight(n((D, U)) * 1.0 / np.sqrt(D) * fd[:, None], "e4m3")
    return {
        "states": (n((D, Q)) * 0.95 / fd[:, None]).astype(np.float32),
        "wq_words": wqp[0],
        "wq_scales": wqp[1],
        "keys_words": keysp[0],
        "keys_scales": keysp[1],
        "notes_words": notesp[0],
        "notes_scales": notesp[1],
        "offs": striped8(idx),
        "offs2": striped8(idx2),
        "offs3": striped8(idx3),
        "offs4": striped8(idx4),
        "offs5": striped8(idx5),
        "offs6": striped8(idx6),
    }


def reference(states, wq_words, wq_scales, keys_words, keys_scales, notes_words, notes_scales, offs, offs2, offs3, offs4, offs5, offs6):
    idx = unstriped8(offs)
    idx2 = unstriped8(offs2)
    idx3 = unstriped8(offs3)
    idx4 = unstriped8(offs4)
    idx5 = unstriped8(offs5)
    idx6 = unstriped8(offs6)
    wqu = unpack_weight(wq_words, wq_scales, "e4m3")
    keysu = unpack_weight(keys_words, keys_scales, "e2m1")
    notesu = unpack_weight(notes_words, notes_scales, "e4m3")
    statesq = mxq(f64(states), 0, "e4m3")
    qv = wqu.T @ statesq
    qvq = mxq(qv, 0, "e4m3")
    a = qvq.T @ keysu
    b = statesq.T @ notesu
    f1 = np.zeros((Q, U))
    f1[np.arange(Q)[:, None], idx2[np.arange(Q) % 128 // 16]] = pick8(a, idx, 16)
    bb = b + f1
    f2 = np.zeros((Q, T))
    f2[np.arange(Q)[:, None], idx4[np.arange(Q) % 128 // 16]] = pick8(bb, idx3, 16)
    f3 = np.zeros((Q, T))
    f3[np.arange(Q)[:, None], idx6[np.arange(Q) % 128 // 16]] = pick8(bb, idx5, 16)
    m1 = np.maximum(f2, f3)
    aa = a - m1
    y = pick8(aa, idx, 16)
    return y

@@ -1,0 +1,183 @@
+from contextlib import ExitStack
+
+import concourse.mybir as mybir
+
+D, K, T, U, I, Q = 512, 512, 1024, 1024, 512, 128
+FLOPS = 2 * (D * K * Q + K * Q * T + D * Q * U)
+
+F32 = mybir.dt.float32
+BF16 = mybir.dt.bfloat16
+I32 = mybir.dt.int32
+U32 = mybir.dt.uint32
+U16 = mybir.dt.uint16
+U8 = mybir.dt.uint8
+FP8X4 = mybir.dt.float8_e4m3fn_x4
+FP4X4 = mybir.dt.float4_e2m1fn_x4
+ALU = mybir.AluOpType
+COPY = mybir.ActivationFunctionType.Copy
+
+P = 128
+PACK = 4
+HALF = I // 2
+PER_COL = 16
+
+
+def tile_attend_tworelays_madeside_kernel(
+    tc, states, wq_words, wq_scales, keys_words, keys_scales, notes_words, notes_scales,
+    offs, offs2, offs3, offs4, offs5, offs6, out,
+):
+    nc = tc.nc
+    with ExitStack() as ctx:
+        sb = ctx.enter_context(tc.tile_pool(name="sb", bufs=1))
+        ps = ctx.enter_context(tc.psum_pool(name="ps", bufs=1))
+
+        def load_scale_rows(queue, plane, rows):
+            for r in range(4):
+                queue.dma_start(out=plane[r:P:32, :].bitcast(I32), in_=rows[0, r:16:4, :].bitcast(I32))
+
+        def load_list(src, name):
+            tile = sb.tile([P, I // PER_COL], U16, name=name)
+            nc.sync.dma_start(tile[:], src)
+            return tile
+
+        def half_of(lst, h):
+            return lst[:, h * HALF // PER_COL : (h + 1) * HALF // PER_COL]
+
+        wq_sc_raw = sb.tile([P, K], U8, name="wq_sc_raw", align_bytes=64)
+        keys_sc = sb.tile([P, T], U8, name="keys_sc", align_bytes=64)
+        notes_sc = sb.tile([P, U], U8, name="notes_sc", align_bytes=64)
+        nc.gpsimd.memset(wq_sc_raw[:].bitcast(I32), 0)
+        nc.gpsimd.memset(keys_sc[:].bitcast(I32), 0)
+        nc.gpsimd.memset(notes_sc[:].bitcast(I32), 0)
+
+        states_raw = sb.tile([P, PACK, Q], F32, name="states_raw")
+        nc.sync.dma_start(out=states_raw[:], in_=states.rearrange("(p j) q -> p j q", j=PACK))
+        wq_raw = sb.tile([P, K], U32, name="wq_raw")
+        nc.sync.dma_start(out=wq_raw[:].bitcast(I32), in_=wq_words[0].rearrange("p n t -> p (n t)").bitcast(I32))
+        load_scale_rows(nc.sync, wq_sc_raw, wq_scales)
+        keys_w = sb.tile([P, 2 * T], U8, name="keys_w", align_bytes=64)
+        nc.sync.dma_start(out=keys_w[:].bitcast(I32), in_=keys_words[0].bitcast(I32))
+        load_scale_rows(nc.sync, keys_sc, keys_scales)
+        l1 = load_list(offs, "l1")
+        l2 = load_list(offs2, "l2")
+        notes_w = sb.tile([P, U], U32, name="notes_w", align_bytes=64)
+        nc.sync.dma_start(out=notes_w[:].bitcast(I32), in_=notes_words[0].rearrange("p n t -> p (n t)").bitcast(I32))
+        load_scale_rows(nc.sync, notes_sc, notes_scales)
+        l3 = load_list(offs3, "l3")
+        l4 = load_list(offs4, "l4")
+        l5 = load_list(offs5, "l5")
+        l6 = load_list(offs6, "l6")
+
+        f1 = sb.tile([P, U], F32, name="f1")
+        f2 = sb.tile([P, T], F32, name="f2")
+        f3 = sb.tile([P, T], F32, name="f3")
+        nc.vector.memset(f1[:], 0.0)
+        nc.vector.memset(f2[:], 0.0)
+        nc.vector.memset(f3[:], 0.0)
+
+        states_bf = sb.tile([P, Q, PACK], BF16, name="states_bf", align_bytes=64)
+        nc.vector.tensor_copy(
+            out=states_bf[:].rearrange("p (c i) t -> p c t i", i=4),
+            in_=states_raw[:].rearrange("p t (c i) -> p c t i", i=4),
+        )
+        wq_w = sb.tile([P, PACK, P], U32, name="wq_w", align_bytes=64)
+        nc.scalar.copy(
+            out=wq_w[:].rearrange("p t (c i) -> p c t i", i=4),
+            in_=wq_raw[:].rearrange("p (c i t) -> p c t i", i=4, t=PACK),
+        )
+        wq_sc = sb.tile([P, PACK, P], U8, name="wq_sc", align_bytes=64)
+        nc.vector.tensor_copy(
+            out=wq_sc[:].rearrange("p t (c i) -> p c t i", i=16),
+            in_=wq_sc_raw[:].rearrange("p (c i t) -> p c t i", i=16, t=PACK),
+        )
+        states_w = sb.tile([P, Q], U32, name="states_w", align_bytes=64)
+        states_sc = sb.tile([P, Q], U8, name="states_sc", align_bytes=64)
+        nc.vector.quantize_mx(
+            out=states_w[:].bitcast(FP8X4), scales=states_sc[:], in_=states_bf[:].rearrange("p q t -> p (q t)")
+        )
+
+        qv_ps = ps.tile([P, PACK, Q], F32, name="qv_ps")
+        for t in range(PACK):
+            nc.tensor.matmul_mx(
+                out=qv_ps[:, t, :], lhsT=wq_w[:, t, :].bitcast(FP8X4), lhsT_scale=wq_sc[:, t, :],
+                rhs=states_w[:].bitcast(FP8X4), rhs_scale=states_sc[:], start=True, stop=True,
+            )
+        qv_bf = sb.tile([P, Q, PACK], BF16, name="qv_bf", align_bytes=64)
+        nc.vector.tensor_copy(out=qv_bf[:], in_=qv_ps[:].rearrange("p t q -> p q t"))
+        qv_w = sb.tile([P, Q], U32, name="qv_w", align_bytes=64)
+        qv_sc = sb.tile([P, Q], U8, name="qv_sc", align_bytes=64)
+        nc.vector.quantize_mx(
+            out=qv_w[:].bitcast(FP8X4), scales=qv_sc[:], in_=qv_bf[:].rearrange("p q t -> p (q t)")
+        )
+
+        a = sb.tile([P, T], F32, name="a")
+        NA = 256
+        for c in range(T // NA):
+            a_ps = ps.tile([P, NA], F32, name=f"a_ps{c}")
+            nc.tensor.matmul_mx(
+                out=a_ps[:], lhsT=qv_w[:].bitcast(FP8X4), lhsT_scale=qv_sc[:],
+                rhs=keys_w[:, 2 * c * NA : 2 * (c + 1) * NA].bitcast(FP4X4),
+                rhs_scale=keys_sc[:, c * NA : (c + 1) * NA], start=True, stop=True,
+            )
+            if c % 2 == 0:
+                nc.vector.tensor_copy(out=a[:, c * NA : (c + 1) * NA], in_=a_ps[:])
+            else:
+                nc.scalar.activation(a[:, c * NA : (c + 1) * NA], a_ps[:], COPY)
+
+        NB = 512
+        b_ps = []
+        for c in range(U // NB):
+            bank = ps.tile([P, NB], F32, name=f"b_ps{c}")
+            nc.tensor.matmul_mx(
+                out=bank[:], lhsT=states_w[:].bitcast(FP8X4), lhsT_scale=states_sc[:],
+                rhs=notes_w[:, c * NB : (c + 1) * NB].bitcast(FP8X4),
+                rhs_scale=notes_sc[:, c * NB : (c + 1) * NB], start=True, stop=True,
+            )
+            b_ps.append(bank)
+
+        def cols_of(h):
+            return slice(h * HALF, (h + 1) * HALF)
+
+        def gather_vector(picked, window, lst, h):
+            nc.vector.tensor_copy(picked[:, cols_of(h)], window[:].indirect(half_of(lst, h)))
+
+        def gather_scalar(picked, window, lst, h):
+            nc.scalar.activation(picked[:, cols_of(h)], window[:].indirect(half_of(lst, h)), COPY)
+
+        def scatter(window, lst, picked, h):
+            nc.vector.tensor_copy(window[:].indirect(half_of(lst, h)), picked[:, cols_of(h)])
+
+        g1 = sb.tile([P, I], F32, name="g1")
+        gather_vector(g1, a, l1, 0)
+        gather_scalar(g1, a, l1, 1)
+        nc.vector.tensor_copy(f1[:].indirect(l2[:]), g1[:])
+
+        bb = sb.tile([P, U], F32, name="bb")
+        for c in range(U // NB):
+            cols = slice(c * NB, (c + 1) * NB)
+            nc.vector.tensor_tensor(bb[:, cols], b_ps[c][:], f1[:, cols], ALU.add)
+
+        g2 = sb.tile([P, I], F32, name="g2")
+        g3 = sb.tile([P, I], F32, name="g3")
+        gather_vector(g2, bb, l3, 0)
+        gather_scalar(g3, bb, l5, 0)
+        gather_scalar(g2, bb, l3, 1)
+        gather_scalar(g3, bb, l5, 1)
+        for h in range(2):
+            scatter(f2, l4, g2, h)
+            scatter(f3, l6, g3, h)
+
+        m1 = sb.tile([P, T], F32, name="m1")
+        aa = sb.tile([P, T], F32, name="aa")
+        for c in range(2):
+            cols = slice(c * 512, (c + 1) * 512)
+            nc.vector.tensor_tensor(m1[:, cols], f2[:, cols], f3[:, cols], ALU.max)
+        for c in range(2):
+            cols = slice(c * 512, (c + 1) * 512)
+            nc.vector.tensor_tensor(aa[:, cols], a[:, cols], m1[:, cols], ALU.subtract)
+
+        y = sb.tile([P, I], F32, name="y")
+        gather_vector(y, aa, l1, 0)
+        gather_scalar(y, aa, l1, 1)
+        nc.sync.dma_start(out=out[:, cols_of(0)], in_=y[:, cols_of(0)])
+        nc.scalar.dma_start(out=out[:, cols_of(1)], in_=y[:, cols_of(1)])

@@ -54,7 +54,7 @@ def tile_attend_tworelays_madeside_kernel(
         nc.sync.dma_start(out=states_raw[:], in_=states.rearrange("(p j) q -> p j q", j=PACK))
         wq_raw = sb.tile([P, K], U32, name="wq_raw")
         nc.sync.dma_start(out=wq_raw[:].bitcast(I32), in_=wq_words[0].rearrange("p n t -> p (n t)").bitcast(I32))
-        load_scale_rows(nc.sync, wq_sc_raw, wq_scales)
+        load_scale_rows(nc.scalar, wq_sc_raw, wq_scales)
         keys_w = sb.tile([P, 2 * T], U8, name="keys_w", align_bytes=64)
         nc.sync.dma_start(out=keys_w[:].bitcast(I32), in_=keys_words[0].bitcast(I32))
         load_scale_rows(nc.sync, keys_sc, keys_scales)
@@ -69,22 +69,19 @@ def tile_attend_tworelays_madeside_kernel(
         l6 = load_list(offs6, "l6")
 
         f1 = sb.tile([P, U], F32, name="f1")
-        f2 = sb.tile([P, T], F32, name="f2")
-        f3 = sb.tile([P, T], F32, name="f3")
         nc.vector.memset(f1[:], 0.0)
-        nc.vector.memset(f2[:], 0.0)
-        nc.vector.memset(f3[:], 0.0)
 
-        states_bf = sb.tile([P, Q, PACK], BF16, name="states_bf", align_bytes=64)
+        states_bf = sb.tile([P, Q, PACK], BF16, name="states_bf", tag="states_bf_then_f2", align_bytes=64)
         nc.vector.tensor_copy(
             out=states_bf[:].rearrange("p (c i) t -> p c t i", i=4),
             in_=states_raw[:].rearrange("p t (c i) -> p c t i", i=4),
         )
-        wq_w = sb.tile([P, PACK, P], U32, name="wq_w", align_bytes=64)
-        nc.scalar.copy(
-            out=wq_w[:].rearrange("p t (c i) -> p c t i", i=4),
-            in_=wq_raw[:].rearrange("p (c i t) -> p c t i", i=4, t=PACK),
-        )
+        wq_w = [sb.tile([P, 2, P], U32, name=f"wq_w{u}", align_bytes=64) for u in range(2)]
+        for u in range(2):
+            nc.scalar.copy(
+                out=wq_w[u][:].rearrange("p t (c i) -> p c t i", i=4),
+                in_=wq_raw[:].rearrange("p (c i t) -> p c t i", i=4, t=PACK)[:, :, 2 * u : 2 * u + 2, :],
+            )
         wq_sc = sb.tile([P, PACK, P], U8, name="wq_sc", align_bytes=64)
         nc.vector.tensor_copy(
             out=wq_sc[:].rearrange("p t (c i) -> p c t i", i=16),
@@ -96,13 +93,16 @@ def tile_attend_tworelays_madeside_kernel(
             out=states_w[:].bitcast(FP8X4), scales=states_sc[:], in_=states_bf[:].rearrange("p q t -> p (q t)")
         )
 
+        f2 = sb.tile([P, T], F32, name="f2", tag="states_bf_then_f2", align_bytes=64)
+        nc.gpsimd.memset(f2[:], 0.0)
+
         qv_ps = ps.tile([P, PACK, Q], F32, name="qv_ps")
         for t in range(PACK):
             nc.tensor.matmul_mx(
-                out=qv_ps[:, t, :], lhsT=wq_w[:, t, :].bitcast(FP8X4), lhsT_scale=wq_sc[:, t, :],
+                out=qv_ps[:, t, :], lhsT=wq_w[t // 2][:, t % 2, :].bitcast(FP8X4), lhsT_scale=wq_sc[:, t, :],
                 rhs=states_w[:].bitcast(FP8X4), rhs_scale=states_sc[:], start=True, stop=True,
             )
-        qv_bf = sb.tile([P, Q, PACK], BF16, name="qv_bf", align_bytes=64)
+        qv_bf = sb.tile([P, Q, PACK], BF16, name="qv_bf", tag="qv_bf_then_f3", align_bytes=64)
         nc.vector.tensor_copy(out=qv_bf[:], in_=qv_ps[:].rearrange("p t q -> p q t"))
         qv_w = sb.tile([P, Q], U32, name="qv_w", align_bytes=64)
         qv_sc = sb.tile([P, Q], U8, name="qv_sc", align_bytes=64)
@@ -110,19 +110,25 @@ def tile_attend_tworelays_madeside_kernel(
             out=qv_w[:].bitcast(FP8X4), scales=qv_sc[:], in_=qv_bf[:].rearrange("p q t -> p (q t)")
         )
 
+        f3 = sb.tile([P, T], F32, name="f3", tag="qv_bf_then_f3", align_bytes=64)
+        nc.gpsimd.memset(f3[:], 0.0)
+
         a = sb.tile([P, T], F32, name="a")
-        NA = 256
-        for c in range(T // NA):
-            a_ps = ps.tile([P, NA], F32, name=f"a_ps{c}")
+        a_edges = [0, 256, 512, 768, 896, 1024]
+        a_ps = []
+        for c in range(len(a_edges) - 1):
+            lo, hi = a_edges[c], a_edges[c + 1]
+            bank = ps.tile([P, hi - lo], F32, name=f"a_ps{c}")
             nc.tensor.matmul_mx(
-                out=a_ps[:], lhsT=qv_w[:].bitcast(FP8X4), lhsT_scale=qv_sc[:],
-                rhs=keys_w[:, 2 * c * NA : 2 * (c + 1) * NA].bitcast(FP4X4),
-                rhs_scale=keys_sc[:, c * NA : (c + 1) * NA], start=True, stop=True,
+                out=bank[:], lhsT=qv_w[:].bitcast(FP8X4), lhsT_scale=qv_sc[:],
+                rhs=keys_w[:, 2 * lo : 2 * hi].bitcast(FP4X4),
+                rhs_scale=keys_sc[:, lo:hi], start=True, stop=True,
             )
             if c % 2 == 0:
-                nc.vector.tensor_copy(out=a[:, c * NA : (c + 1) * NA], in_=a_ps[:])
+                nc.vector.tensor_copy(out=a[:, lo:hi], in_=bank[:])
             else:
-                nc.scalar.activation(a[:, c * NA : (c + 1) * NA], a_ps[:], COPY)
+                nc.scalar.activation(a[:, lo:hi], bank[:], COPY)
+            a_ps.append(bank)
 
         NB = 512
         b_ps = []
@@ -153,9 +159,12 @@ def tile_attend_tworelays_madeside_kernel(
         nc.vector.tensor_copy(f1[:].indirect(l2[:]), g1[:])
 
         bb = sb.tile([P, U], F32, name="bb")
-        for c in range(U // NB):
-            cols = slice(c * NB, (c + 1) * NB)
-            nc.vector.tensor_tensor(bb[:, cols], b_ps[c][:], f1[:, cols], ALU.add)
+        SPLIT = 704
+        b_tail = sb.tile([P, U - SPLIT], F32, name="b_tail")
+        nc.scalar.activation(b_tail[:], b_ps[1][:, SPLIT - NB :], COPY)
+        nc.gpsimd.tensor_tensor(bb[:, SPLIT:], b_tail[:], f1[:, SPLIT:], ALU.add)
+        nc.vector.tensor_tensor(bb[:, :NB], b_ps[0][:], f1[:, :NB], ALU.add)
+        nc.vector.tensor_tensor(bb[:, NB:SPLIT], b_ps[1][:, : SPLIT - NB], f1[:, NB:SPLIT], ALU.add)
 
         g2 = sb.tile([P, I], F32, name="g2")
         g3 = sb.tile([P, I], F32, name="g3")
@@ -169,12 +178,12 @@ def tile_attend_tworelays_madeside_kernel(
 
         m1 = sb.tile([P, T], F32, name="m1")
         aa = sb.tile([P, T], F32, name="aa")
-        for c in range(2):
-            cols = slice(c * 512, (c + 1) * 512)
+        for cols in (slice(512, T), slice(0, 512)):
             nc.vector.tensor_tensor(m1[:, cols], f2[:, cols], f3[:, cols], ALU.max)
-        for c in range(2):
-            cols = slice(c * 512, (c + 1) * 512)
-            nc.vector.tensor_tensor(aa[:, cols], a[:, cols], m1[:, cols], ALU.subtract)
+        nc.gpsimd.tensor_tensor(aa[:, SPLIT:], a[:, SPLIT:], m1[:, SPLIT:], ALU.subtract)
+        for c in (2, 0, 1):
+            lo, hi = a_edges[c], min(a_edges[c + 1], SPLIT)
+            nc.vector.tensor_tensor(aa[:, lo:hi], a_ps[c][:, : hi - lo], m1[:, lo:hi], ALU.subtract)
 
         y = sb.tile([P, I], F32, name="y")
         gather_vector(y, aa, l1, 0)

@@ -47,14 +47,14 @@ def tile_attend_tworelays_madeside_kernel(
         keys_sc = sb.tile([P, T], U8, name="keys_sc", align_bytes=64)
         notes_sc = sb.tile([P, U], U8, name="notes_sc", align_bytes=64)
         nc.gpsimd.memset(wq_sc_raw[:].bitcast(I32), 0)
-        nc.gpsimd.memset(keys_sc[:].bitcast(I32), 0)
+        nc.vector.memset(keys_sc[:].bitcast(I32), 0)
         nc.gpsimd.memset(notes_sc[:].bitcast(I32), 0)
 
         states_raw = sb.tile([P, PACK, Q], F32, name="states_raw")
         nc.sync.dma_start(out=states_raw[:], in_=states.rearrange("(p j) q -> p j q", j=PACK))
         wq_raw = sb.tile([P, K], U32, name="wq_raw")
         nc.sync.dma_start(out=wq_raw[:].bitcast(I32), in_=wq_words[0].rearrange("p n t -> p (n t)").bitcast(I32))
-        load_scale_rows(nc.scalar, wq_sc_raw, wq_scales)
+        load_scale_rows(nc.sync, wq_sc_raw, wq_scales)
         keys_w = sb.tile([P, 2 * T], U8, name="keys_w", align_bytes=64)
         nc.sync.dma_start(out=keys_w[:].bitcast(I32), in_=keys_words[0].bitcast(I32))
         load_scale_rows(nc.sync, keys_sc, keys_scales)
@@ -76,17 +76,17 @@ def tile_attend_tworelays_madeside_kernel(
             out=states_bf[:].rearrange("p (c i) t -> p c t i", i=4),
             in_=states_raw[:].rearrange("p t (c i) -> p c t i", i=4),
         )
+        wq_sc = sb.tile([P, PACK, P], U8, name="wq_sc", align_bytes=64)
+        nc.vector.tensor_copy(
+            out=wq_sc[:].rearrange("p t (c i) -> p c t i", i=16),
+            in_=wq_sc_raw[:].rearrange("p (c i t) -> p c t i", i=16, t=PACK),
+        )
         wq_w = [sb.tile([P, 2, P], U32, name=f"wq_w{u}", align_bytes=64) for u in range(2)]
         for u in range(2):
             nc.scalar.copy(
                 out=wq_w[u][:].rearrange("p t (c i) -> p c t i", i=4),
                 in_=wq_raw[:].rearrange("p (c i t) -> p c t i", i=4, t=PACK)[:, :, 2 * u : 2 * u + 2, :],
             )
-        wq_sc = sb.tile([P, PACK, P], U8, name="wq_sc", align_bytes=64)
-        nc.vector.tensor_copy(
-            out=wq_sc[:].rearrange("p t (c i) -> p c t i", i=16),
-            in_=wq_sc_raw[:].rearrange("p (c i t) -> p c t i", i=16, t=PACK),
-        )
         states_w = sb.tile([P, Q], U32, name="states_w", align_bytes=64)
         states_sc = sb.tile([P, Q], U8, name="states_sc", align_bytes=64)
         nc.vector.quantize_mx(
@@ -96,14 +96,26 @@ def tile_attend_tworelays_madeside_kernel(
         f2 = sb.tile([P, T], F32, name="f2", tag="states_bf_then_f2", align_bytes=64)
         nc.gpsimd.memset(f2[:], 0.0)
 
-        qv_ps = ps.tile([P, PACK, Q], F32, name="qv_ps")
+        qv_ps = [ps.tile([P, 2, Q], F32, name=f"qv_ps{u}") for u in range(2)]
         for t in range(PACK):
             nc.tensor.matmul_mx(
-                out=qv_ps[:, t, :], lhsT=wq_w[t // 2][:, t % 2, :].bitcast(FP8X4), lhsT_scale=wq_sc[:, t, :],
+                out=qv_ps[t // 2][:, t % 2, :], lhsT=wq_w[t // 2][:, t % 2, :].bitcast(FP8X4), lhsT_scale=wq_sc[:, t, :],
                 rhs=states_w[:].bitcast(FP8X4), rhs_scale=states_sc[:], start=True, stop=True,
             )
+        NB = 512
+
+        def score_notes(c, tag):
+            bank = ps.tile([P, NB], F32, name=f"b_ps{c}", tag=tag)
+            nc.tensor.matmul_mx(
+                out=bank[:], lhsT=states_w[:].bitcast(FP8X4), lhsT_scale=states_sc[:],
+                rhs=notes_w[:, c * NB : (c + 1) * NB].bitcast(FP8X4),
+                rhs_scale=notes_sc[:, c * NB : (c + 1) * NB], start=True, stop=True,
+            )
+            return bank
+
         qv_bf = sb.tile([P, Q, PACK], BF16, name="qv_bf", tag="qv_bf_then_f3", align_bytes=64)
-        nc.vector.tensor_copy(out=qv_bf[:], in_=qv_ps[:].rearrange("p t q -> p q t"))
+        nc.scalar.copy(out=qv_bf[:, :, 0:2], in_=qv_ps[0][:].rearrange("p t q -> p q t"))
+        nc.vector.tensor_copy(out=qv_bf[:, :, 2:4], in_=qv_ps[1][:].rearrange("p t q -> p q t"))
         qv_w = sb.tile([P, Q], U32, name="qv_w", align_bytes=64)
         qv_sc = sb.tile([P, Q], U8, name="qv_sc", align_bytes=64)
         nc.vector.quantize_mx(
@@ -130,16 +142,7 @@ def tile_attend_tworelays_madeside_kernel(
                 nc.scalar.activation(a[:, lo:hi], bank[:], COPY)
             a_ps.append(bank)
 
-        NB = 512
-        b_ps = []
-        for c in range(U // NB):
-            bank = ps.tile([P, NB], F32, name=f"b_ps{c}")
-            nc.tensor.matmul_mx(
-                out=bank[:], lhsT=states_w[:].bitcast(FP8X4), lhsT_scale=states_sc[:],
-                rhs=notes_w[:, c * NB : (c + 1) * NB].bitcast(FP8X4),
-                rhs_scale=notes_sc[:, c * NB : (c + 1) * NB], start=True, stop=True,
-            )
-            b_ps.append(bank)
+        b_ps = [score_notes(0, "a_ps3"), score_notes(1, "a_ps4")]
 
         def cols_of(h):
             return slice(h * HALF, (h + 1) * HALF)

@@ -114,8 +114,8 @@ def tile_attend_tworelays_madeside_kernel(
             return bank
 
         qv_bf = sb.tile([P, Q, PACK], BF16, name="qv_bf", tag="qv_bf_then_f3", align_bytes=64)
-        nc.scalar.copy(out=qv_bf[:, :, 0:2], in_=qv_ps[0][:].rearrange("p t q -> p q t"))
-        nc.vector.tensor_copy(out=qv_bf[:, :, 2:4], in_=qv_ps[1][:].rearrange("p t q -> p q t"))
+        nc.vector.tensor_copy(out=qv_bf[:, :, 0:2], in_=qv_ps[0][:].rearrange("p t q -> p q t"))
+        nc.scalar.copy(out=qv_bf[:, :, 2:4], in_=qv_ps[1][:].rearrange("p t q -> p q t"))
         qv_w = sb.tile([P, Q], U32, name="qv_w", align_bytes=64)
         qv_sc = sb.tile([P, Q], U8, name="qv_sc", align_bytes=64)
         nc.vector.quantize_mx(
@@ -181,10 +181,10 @@ def tile_attend_tworelays_madeside_kernel(
 
         m1 = sb.tile([P, T], F32, name="m1")
         aa = sb.tile([P, T], F32, name="aa")
-        for cols in (slice(512, T), slice(0, 512)):
+        for cols in (slice(256, T), slice(0, 256)):
             nc.vector.tensor_tensor(m1[:, cols], f2[:, cols], f3[:, cols], ALU.max)
         nc.gpsimd.tensor_tensor(aa[:, SPLIT:], a[:, SPLIT:], m1[:, SPLIT:], ALU.subtract)
-        for c in (2, 0, 1):
+        for c in (2, 1, 0):
             lo, hi = a_edges[c], min(a_edges[c + 1], SPLIT)
             nc.vector.tensor_tensor(aa[:, lo:hi], a_ps[c][:, : hi - lo], m1[:, lo:hi], ALU.subtract)
 
@@ -192,4 +192,4 @@ def tile_attend_tworelays_madeside_kernel(
         gather_vector(y, aa, l1, 0)
         gather_scalar(y, aa, l1, 1)
         nc.sync.dma_start(out=out[:, cols_of(0)], in_=y[:, cols_of(0)])
-        nc.scalar.dma_start(out=out[:, cols_of(1)], in_=y[:, cols_of(1)])
+        nc.sync.dma_start(out=out[:, cols_of(1)], in_=y[:, cols_of(1)])

from contextlib import ExitStack

import concourse.mybir as mybir

D, K, T, U, I, Q = 512, 512, 1024, 1024, 512, 128
FLOPS = 2 * (D * K * Q + K * Q * T + D * Q * U)

F32 = mybir.dt.float32
BF16 = mybir.dt.bfloat16
I32 = mybir.dt.int32
U32 = mybir.dt.uint32
U16 = mybir.dt.uint16
U8 = mybir.dt.uint8
FP8X4 = mybir.dt.float8_e4m3fn_x4
FP4X4 = mybir.dt.float4_e2m1fn_x4
ALU = mybir.AluOpType
COPY = mybir.ActivationFunctionType.Copy

P = 128
PACK = 4
HALF = I // 2
PER_COL = 16


def tile_attend_tworelays_madeside_kernel(
    tc, states, wq_words, wq_scales, keys_words, keys_scales, notes_words, notes_scales,
    offs, offs2, offs3, offs4, offs5, offs6, out,
):
    nc = tc.nc
    with ExitStack() as ctx:
        sb = ctx.enter_context(tc.tile_pool(name="sb", bufs=1))
        ps = ctx.enter_context(tc.psum_pool(name="ps", bufs=1))

        def load_scale_rows(queue, plane, rows):
            for r in range(4):
                queue.dma_start(out=plane[r:P:32, :].bitcast(I32), in_=rows[0, r:16:4, :].bitcast(I32))

        def load_list(src, name):
            tile = sb.tile([P, I // PER_COL], U16, name=name)
            nc.sync.dma_start(tile[:], src)
            return tile

        def half_of(lst, h):
            return lst[:, h * HALF // PER_COL : (h + 1) * HALF // PER_COL]

        wq_sc_raw = sb.tile([P, K], U8, name="wq_sc_raw", align_bytes=64)
        keys_sc = sb.tile([P, T], U8, name="keys_sc", align_bytes=64)
        notes_sc = sb.tile([P, U], U8, name="notes_sc", align_bytes=64)
        nc.gpsimd.memset(wq_sc_raw[:].bitcast(I32), 0)
        nc.vector.memset(keys_sc[:].bitcast(I32), 0)
        nc.gpsimd.memset(notes_sc[:].bitcast(I32), 0)

        states_raw = sb.tile([P, PACK, Q], F32, name="states_raw")
        nc.sync.dma_start(out=states_raw[:], in_=states.rearrange("(p j) q -> p j q", j=PACK))
        wq_raw = sb.tile([P, K], U32, name="wq_raw")
        nc.sync.dma_start(out=wq_raw[:].bitcast(I32), in_=wq_words[0].rearrange("p n t -> p (n t)").bitcast(I32))
        load_scale_rows(nc.sync, wq_sc_raw, wq_scales)
        keys_w = sb.tile([P, 2 * T], U8, name="keys_w", align_bytes=64)
        nc.sync.dma_start(out=keys_w[:].bitcast(I32), in_=keys_words[0].bitcast(I32))
        load_scale_rows(nc.sync, keys_sc, keys_scales)
        l1 = load_list(offs, "l1")
        l2 = load_list(offs2, "l2")
        notes_w = sb.tile([P, U], U32, name="notes_w", align_bytes=64)
        nc.sync.dma_start(out=notes_w[:].bitcast(I32), in_=notes_words[0].rearrange("p n t -> p (n t)").bitcast(I32))
        load_scale_rows(nc.sync, notes_sc, notes_scales)
        l3 = load_list(offs3, "l3")
        l4 = load_list(offs4, "l4")
        l5 = load_list(offs5, "l5")
        l6 = load_list(offs6, "l6")

        f1 = sb.tile([P, U], F32, name="f1")
        nc.vector.memset(f1[:], 0.0)

        states_bf = sb.tile([P, Q, PACK], BF16, name="states_bf", tag="states_bf_then_f2", align_bytes=64)
        nc.vector.tensor_copy(
            out=states_bf[:].rearrange("p (c i) t -> p c t i", i=4),
            in_=states_raw[:].rearrange("p t (c i) -> p c t i", i=4),
        )
        wq_sc = sb.tile([P, PACK, P], U8, name="wq_sc", align_bytes=64)
        nc.vector.tensor_copy(
            out=wq_sc[:].rearrange("p t (c i) -> p c t i", i=16),
            in_=wq_sc_raw[:].rearrange("p (c i t) -> p c t i", i=16, t=PACK),
        )
        wq_w = [sb.tile([P, 2, P], U32, name=f"wq_w{u}", align_bytes=64) for u in range(2)]
        for u in range(2):
            nc.scalar.copy(
                out=wq_w[u][:].rearrange("p t (c i) -> p c t i", i=4),
                in_=wq_raw[:].rearrange("p (c i t) -> p c t i", i=4, t=PACK)[:, :, 2 * u : 2 * u + 2, :],
            )
        states_w = sb.tile([P, Q], U32, name="states_w", align_bytes=64)
        states_sc = sb.tile([P, Q], U8, name="states_sc", align_bytes=64)
        nc.vector.quantize_mx(
            out=states_w[:].bitcast(FP8X4), scales=states_sc[:], in_=states_bf[:].rearrange("p q t -> p (q t)")
        )

        f2 = sb.tile([P, T], F32, name="f2", tag="states_bf_then_f2", align_bytes=64)
        nc.gpsimd.memset(f2[:], 0.0)

        qv_ps = [ps.tile([P, 2, Q], F32, name=f"qv_ps{u}") for u in range(2)]
        for t in range(PACK):
            nc.tensor.matmul_mx(
                out=qv_ps[t // 2][:, t % 2, :], lhsT=wq_w[t // 2][:, t % 2, :].bitcast(FP8X4), lhsT_scale=wq_sc[:, t, :],
                rhs=states_w[:].bitcast(FP8X4), rhs_scale=states_sc[:], start=True, stop=True,
            )
        NB = 512

        def score_notes(c, tag):
            bank = ps.tile([P, NB], F32, name=f"b_ps{c}", tag=tag)
            nc.tensor.matmul_mx(
                out=bank[:], lhsT=states_w[:].bitcast(FP8X4), lhsT_scale=states_sc[:],
                rhs=notes_w[:, c * NB : (c + 1) * NB].bitcast(FP8X4),
                rhs_scale=notes_sc[:, c * NB : (c + 1) * NB], start=True, stop=True,
            )
            return bank

        qv_bf = sb.tile([P, Q, PACK], BF16, name="qv_bf", tag="qv_bf_then_f3", align_bytes=64)
        nc.vector.tensor_copy(out=qv_bf[:, :, 0:2], in_=qv_ps[0][:].rearrange("p t q -> p q t"))
        nc.scalar.copy(out=qv_bf[:, :, 2:4], in_=qv_ps[1][:].rearrange("p t q -> p q t"))
        qv_w = sb.tile([P, Q], U32, name="qv_w", align_bytes=64)
        qv_sc = sb.tile([P, Q], U8, name="qv_sc", align_bytes=64)
        nc.vector.quantize_mx(
            out=qv_w[:].bitcast(FP8X4), scales=qv_sc[:], in_=qv_bf[:].rearrange("p q t -> p (q t)")
        )

        f3 = sb.tile([P, T], F32, name="f3", tag="qv_bf_then_f3", align_bytes=64)
        nc.gpsimd.memset(f3[:], 0.0)

        a = sb.tile([P, T], F32, name="a")
        a_edges = [0, 256, 512, 768, 896, 1024]
        a_ps = []
        for c in range(len(a_edges) - 1):
            lo, hi = a_edges[c], a_edges[c + 1]
            bank = ps.tile([P, hi - lo], F32, name=f"a_ps{c}")
            nc.tensor.matmul_mx(
                out=bank[:], lhsT=qv_w[:].bitcast(FP8X4), lhsT_scale=qv_sc[:],
                rhs=keys_w[:, 2 * lo : 2 * hi].bitcast(FP4X4),
                rhs_scale=keys_sc[:, lo:hi], start=True, stop=True,
            )
            if c % 2 == 0:
                nc.vector.tensor_copy(out=a[:, lo:hi], in_=bank[:])
            else:
                nc.scalar.activation(a[:, lo:hi], bank[:], COPY)
            a_ps.append(bank)

        b_ps = [score_notes(0, "a_ps3"), score_notes(1, "a_ps4")]

        def cols_of(h):
            return slice(h * HALF, (h + 1) * HALF)

        def gather_vector(picked, window, lst, h):
            nc.vector.tensor_copy(picked[:, cols_of(h)], window[:].indirect(half_of(lst, h)))

        def gather_scalar(picked, window, lst, h):
            nc.scalar.activation(picked[:, cols_of(h)], window[:].indirect(half_of(lst, h)), COPY)

        def scatter(window, lst, picked, h):
            nc.vector.tensor_copy(window[:].indirect(half_of(lst, h)), picked[:, cols_of(h)])

        g1 = sb.tile([P, I], F32, name="g1")
        gather_vector(g1, a, l1, 0)
        gather_scalar(g1, a, l1, 1)
        nc.vector.tensor_copy(f1[:].indirect(l2[:]), g1[:])

        bb = sb.tile([P, U], F32, name="bb")
        SPLIT = 704
        b_tail = sb.tile([P, U - SPLIT], F32, name="b_tail")
        nc.scalar.activation(b_tail[:], b_ps[1][:, SPLIT - NB :], COPY)
        nc.gpsimd.tensor_tensor(bb[:, SPLIT:], b_tail[:], f1[:, SPLIT:], ALU.add)
        nc.vector.tensor_tensor(bb[:, :NB], b_ps[0][:], f1[:, :NB], ALU.add)
        nc.vector.tensor_tensor(bb[:, NB:SPLIT], b_ps[1][:, : SPLIT - NB], f1[:, NB:SPLIT], ALU.add)

        g2 = sb.tile([P, I], F32, name="g2")
        g3 = sb.tile([P, I], F32, name="g3")
        gather_vector(g2, bb, l3, 0)
        gather_scalar(g3, bb, l5, 0)
        gather_scalar(g2, bb, l3, 1)
        gather_scalar(g3, bb, l5, 1)
        for h in range(2):
            scatter(f2, l4, g2, h)
            scatter(f3, l6, g3, h)

        m1 = sb.tile([P, T], F32, name="m1")
        aa = sb.tile([P, T], F32, name="aa")
        for cols in (slice(256, T), slice(0, 256)):
            nc.vector.tensor_tensor(m1[:, cols], f2[:, cols], f3[:, cols], ALU.max)
        nc.gpsimd.tensor_tensor(aa[:, SPLIT:], a[:, SPLIT:], m1[:, SPLIT:], ALU.subtract)
        for c in (2, 1, 0):
            lo, hi = a_edges[c], min(a_edges[c + 1], SPLIT)
            nc.vector.tensor_tensor(aa[:, lo:hi], a_ps[c][:, : hi - lo], m1[:, lo:hi], ALU.subtract)

        y = sb.tile([P, I], F32, name="y")
        gather_vector(y, aa, l1, 0)
        gather_scalar(y, aa, l1, 1)
        nc.sync.dma_start(out=out[:, cols_of(0)], in_=y[:, cols_of(0)])
        nc.sync.dma_start(out=out[:, cols_of(1)], in_=y[:, cols_of(1)])
